import numpy as np, ml_dtypes
CORES = [2,3,42,43,82,83,122,123]
N = 8
T, EL, CAP, CAPP = 4096, 4, 960, 256
E = N * EL
def entries(a): return a.T.reshape(-1)
def pack(v, P): return np.ascontiguousarray(np.asarray(v, np.int32).reshape(-1, P).T)
def lists(rng, how):
    g, q, h, R, K = CAP // CAPP, CAP % CAPP, E // 4, np.arange(N)[:, None], np.arange(E)
    C = np.zeros((N, E), np.int64); s = rng.integers(1, E, N); S = None
    few = rng.integers(1, CAPP // 4 + 1, (N, h)); t = rng.integers(CAPP // 8, 3 * CAPP // 8 + 1, (N, 3)); t[:, 2] = CAPP - t[:, 0] - t[:, 1]
    if how == "uniform":
        C[:, :h] = np.where(R <= g, CAPP, few); C[:, h:] = rng.integers(0, CAP // (2 * N) + 1, (N, E - h)); S = np.stack([rng.permutation(2 * h)[:3] + 1 for r in range(N)])
    if how == "bands":
        a = np.arange(E) % N; C = CAPP * ((R >= a) & (R <= a + g)); C[a[N:], np.arange(N, E)] = rng.integers(1, CAPP + 1, E - N); s[g:] = N - g + rng.integers(0, g, N - g) - np.arange(N - g)
    if how == "full":
        v = rng.integers(CAPP - q + 1, CAPP, h + 1); C[:, :h] = CAPP; C[:, h:2 * h + 1] = (CAP - v) // N; C[rng.integers(N), h:2 * h + 1] += (CAP - v) % N; s = h + (np.arange(N) + rng.integers(2)) % 2
    if how == "late":
        C[:N - 1, :h] = np.where(R <= g, CAPP, few)[:N - 1]; C[N - 1, h:3 * h] = rng.integers(1, CAPP + 1, 2 * h); s = rng.integers(h, 2 * h + 1, N)
    if how == "mesh":
        ev = np.arange(0, E, 2); P = np.stack([rng.permutation(2 * h) for r in range(N)]); S = 2 * P[:, :3] + 1; S[g] = 2 * rng.permutation(2 * h - 1)[:3] + 2
        C[:, ev] = CAPP; C[g, ev[h:]] = q; C[g, ev + 1] = rng.integers(0, (CAPP - q) // 2 + 1, 2 * h); C[g, 1] = 0
        z, y = g + 1 + int(rng.integers(0, g - 1)), 2 * int(rng.integers(1, 2 * h)) + 1; C[z, (y - 2 * P[z, 3] - 1) % E] = 0; C[z, y] = CAPP
    if how == "thin":
        C = rng.integers(0, CAP // N + 1, (N, E)); C[1] = 1; C[[0, N // 2, N - 1]] = 0
    if S is None: S, t = s[:, None], np.full((N, 1), CAPP)
    D = np.zeros((N, E, E), np.int64); Z = C.copy()
    for j in range(S.shape[1]):
        w = rng.integers(np.maximum(Z - t[:, j + 1:].sum(axis=1)[:, None], 0), np.minimum(Z, t[:, j:j + 1]) + 1); D[R, K, (K + S[:, j:j + 1]) % E] = w; Z -= w
    X = np.stack([rng.permutation(np.concatenate([np.repeat(np.arange(E * E), D[r].reshape(-1)), np.full(T - D[r].sum(), -1)])) for r in range(N)]); c = np.append(rng.permutation(E), -1)
    return {"e1": np.stack([pack(w, 16) for w in c[X // E]]), "e2": np.stack([pack(w, 16) for w in c[np.where(X < 0, -1, X % E)]])}
def blank(d):
    for r in range(0, N, 2):
        u, i = np.unique(entries(d["e1"][r])[::-1], return_index=True); d["x"][r][:, T - 1 - i[u >= 0]] = 0
def setup_inputs(rng):
    return dict({"x": rng.standard_normal((N, 128, T), dtype=np.float32).astype(ml_dtypes.bfloat16)}, **lists(rng, "uniform"))
def setup_inputs_bands(rng):
    d = setup_inputs(rng); d.update(lists(rng, "bands"))
    for k in ("x",): d[k] = (d[k].astype(np.float32) * 1048576.0).astype(d[k].dtype)
    blank(d)
    return d
def setup_inputs_full(rng):
    d = setup_inputs(rng); d.update(lists(rng, "full"))
    for k in ("x",): d[k] = (d[k].astype(np.float32) * (1 / 1024.0)).astype(d[k].dtype)
    blank(d)
    return d
def setup_inputs_late(rng):
    d = setup_inputs(rng); d.update(lists(rng, "late"))
    blank(d)
    return d
def setup_inputs_mesh(rng):
    d = setup_inputs(rng); d.update(lists(rng, "mesh"))
    blank(d)
    return d
def setup_inputs_thin(rng):
    d = setup_inputs(rng); d.update(lists(rng, "thin"))
    blank(d)
    return d
def check_inputs(x):
    bad = []; a, b = x["e1"], x["e2"]
    if min(a.min(), b.min()) < -1 or max(a.max(), b.max()) >= E: bad.append("e1 or e2 out of range")
    if ((a < 0) != (b < 0)).any(): bad.append("-1 stands in one of e1 and e2 alone")
    if ((a == b) & (a >= 0)).any(): bad.append("a token's two choices are one expert")
    if max(int(np.bincount(v[v >= 0], minlength=E).max()) for w in (a, b) for v in w) > CAPP: bad.append("more than CAPP tokens of one rank have one expert as first choice, or as second choice")
    return bad
def places(e):
    o = np.argsort(e, kind="stable"); p = np.empty(len(e), np.int64); p[o] = np.arange(len(e)) - np.searchsorted(e[o], e[o]); return p
def reference(x, e1, e2):
    X = np.concatenate(list(x), axis=1); a, b = [np.concatenate([entries(v) for v in w]) for w in (e1, e2)]
    k = np.nonzero(a >= 0)[0]; p = places(a[k])
    c1 = np.minimum(np.bincount(a[k], minlength=E), CAP)
    f = k[p >= CAP]; u = c1[b[f]] + places(b[f])
    Y = np.zeros((128, E * CAP), x.dtype); m = p < CAP; Y[:, CAP * a[k[m]] + p[m]] = X[:, k[m]]
    n = u < CAP; Y[:, CAP * b[f[n]] + u[n]] = X[:, f[n]]
    return {"y": np.stack([Y[:, EL * CAP * r:EL * CAP * (r + 1)] for r in range(N)])}

@@ -1,0 +1,427 @@
+from concourse.bass import DstId, RemoteDMATransfer
+from concourse.mybir import AluOpType as Op, ActivationFunctionType as Act
+
+NC, N, NT, EL, CAP, CAPP = 128, 8, 4096, 4, 960, 256
+FIRST2 = CAP // CAPP
+BLK = EL * CAPP
+NSEG = N + N - FIRST2
+ZERO = NSEG * BLK
+PIECES = [[(0, 1088), (1088, 2176)], [(2176, 3136), (3136, 4096)]]
+RW = 1088
+PB = 264
+NTOK8, SLOTS = NT // 8, 8 * CAPP
+
+SCRATCH = {"p%d" % _i: ("psum", [128, 512], "float32") for _i in range(8)}
+for _d, _b in (
+    ("bfloat16", dict(
+        xw=NT, rl=2 * RW,
+        pk=ZERO + CAP, ys=EL * CAP, ob=4 * BLK,
+        cl=4, ld1=4 * N, cl2=2, ld2=2 * N,
+        colA=144, colG=128, colX=240, colT=256, colH=128, rg=1024, bo=128, rep=128, gt=128, u1=128, wd=144, wide=240, wideW=240,
+        mapd=128, repq=1024, dat=NTOK8, lb=64, o1=1024, m1=1024, ps=4 * PB, ps2=PB, hh=256, o2=256, m2=256, thr=512,
+        win1=NTOK8 + SLOTS, win2=NTOK8 + SLOTS, hl=60)),
+    ("float32", dict(sc=64, trash=32, tf=64, cap=NSEG, bq=NSEG + 1, db=NSEG, dl=NSEG, tb=30 * NSEG + 420)),
+    ("int32", dict(le=64, pi=1, ia=8)),
+    ("uint16", dict(to1=32, to2=32, off1=SLOTS // 16, off2=SLOTS // 16, offF=EL * CAP // 16)),
+):
+    SCRATCH.update({_n: ("sbuf", [128, _w], _d) for _n, _w in _b.items()})
+SEMAPHORES = ["lst", "xin", "c1a", "c1b", "c2", "pin", "rel0", "rel1", "sent"] + ["s%d" % i for i in range(130)]
+
+
+def plan(T, topo):
+    cores = list(T.cores)
+    chips = []
+    for c in cores:
+        if topo.chip(c) not in chips:
+            chips.append(topo.chip(c))
+    on = {}
+    for c in range(NC):
+        on.setdefault(topo.chip(c), []).append(c)
+    server, relay, mrel = {}, {}, {}
+    for X in chips:
+        own = [c for c in cores if topo.chip(c) == X]
+        free = [c for c in on[X] if c not in own]
+        for r, c in enumerate(cores):
+            server[X, r] = c if c in own else free.pop(0)
+        cand = [c for c in on[X] if topo.die(c) != topo.die(own[0]) and all(topo.may_write(c, d) for d in cores if topo.chip(d) != X)]
+        for i, c in enumerate(own):
+            relay[c] = cand[i]
+    for X in chips:
+        M = [m for m in on if topo.mates(X, m)][0]
+        far = [A for A in chips if A != X and not topo.same_plane(A, X)]
+        for k, A in enumerate(far):
+            for i, c in enumerate([c for c in cores if topo.chip(c) == A]):
+                for part, s in enumerate((c, relay[c])):
+                    own = [m for m in on[M] if topo.die(m) == topo.die(s) and topo.may_write(m, server[X, cores.index(c)])]
+                    mrel[X, cores.index(c), part] = (own[i], k)
+    return cores, chips, server, relay, mrel
+
+
+def rank_program(g, core, T, topo):
+    cores, chips, server, relay, mrel = plan(T, topo)
+    X = topo.chip(core)
+    bits = lambda m: bin(m).count("1")
+    sent = [0]
+
+    def write(dsts, out, in_, rsem, mask):
+        ids = [topo.addr(d) for d in dsts]
+        if len(dsts) == 1:
+            g.remote_dma(out, in_, T.sem[rsem], T.sem.sent, pid=ids[0][1], routing_id=ids[0][0], dma_engine_mask=mask)
+        elif dsts:
+            g.remote_dma_fused([RemoteDMATransfer(dst_ids=[DstId(rid=a[0], pnc=a[1]) for a in ids], dma_engine_mask=mask, remote_sem=T.sem[rsem],
+                                                  srcs=[in_], dsts=[out for _ in dsts])], local_sem=T.sem.sent)
+        sent[0] += bits(mask) if dsts else 0
+
+    if X not in chips:
+        for k, q, Y, part in sorted((mrel[key][1], key[1], key[0], key[2]) for key in mrel if mrel[key][0] == core):
+            a, b = PIECES[part][0]
+            OFF = topo.mask(core, server[Y, q])
+            g.wait_ge(T.sem["rel%d" % k], bits(OFF))
+            write([server[Y, q]], T.xw[:, a:b], T.rl[:, RW * k:RW * k + b - a], "xin", OFF)
+        if sent[0]:
+            g.wait_ge(T.sem.sent, sent[0])
+        return
+
+    x = chips.index(X)
+    r = [q for q in range(N) if server[X, q] == core][0]
+    dests = [c for c in cores if topo.chip(c) == X]
+    isr = core in dests
+    dloc = dests.index(core) if isr else None
+    asks = r >= FIRST2
+    others = [Y for Y in chips if Y != X]
+    ON = topo.mask(core, [c for c in dests if c != core][0])
+    OFF = topo.mask(core, server[others[0], 0])
+    HI = ON & ~OFF
+    busy = lambda c: c in dests or c in [relay[d] for d in dests]
+    cmask = lambda c: HI if busy(c) else ON
+    v, pe, sa, sy = g.vector, g.tensor, g.scalar, g.sync
+
+    num, cnt, seen = {}, {}, {}
+
+    def did(ins, nm, n=1):
+        if nm not in num:
+            num[nm] = len(num)
+            cnt[nm] = 0
+        ins.then_inc(T.sem["s%d" % num[nm]], n)
+        cnt[nm] += n
+
+    def need(q, k, *names):
+        for nm in names:
+            if seen.get((k, nm)) != cnt[nm]:
+                q.wait_ge(T.sem["s%d" % num[nm]], cnt[nm])
+                seen[k, nm] = cnt[nm]
+
+    def vn(*a): need(v, "v", *a)
+    def pn(*a): need(pe, "p", *a)
+    def gn(*a): need(g, "g", *a)
+
+    flat = [(1, 0), (1, 1), (0, 0), (0, 1)]
+    if isr:
+        did(sy.dma_start(T.le[:, 0:32], T.e1[:]), "le", 16)
+        did(sa.dma_start(T.le[:, 32:64], T.e2[:]), "le", 16)
+        for i, (p, j) in enumerate(flat):
+            a, b = PIECES[p][j]
+            did((sy if i % 2 == 0 else sa).dma_start(T.xw[:, a:b], T.x[:, a:b]), "x%d%d" % (p, j), 16)
+
+    row = dict(allow_small_or_imprecise_dtypes=True)
+    did(g.iota(T.pi[:], [[0, 1]], 0, 1), "pi")
+    did(g.iota(T.colX[:], [[1, 240]], -112, 0, **row), "colX")
+    did(g.iota(T.colA[:], [[0, 9], [1, 16]], 0, 0, **row), "colA")
+    did(g.iota(T.colG[:], [[1, 8], [0, 16]], 0, 0, **row), "colG")
+
+    def out_piece(q, part, j, src):
+        a, b = PIECES[part][j]
+        via = [mrel[Y, q, part] for Y in others if (Y, q, part) in mrel] if j == 0 else []
+        if via:
+            k = via[0][1]
+            write([m[0] for m in via], T.rl[:, RW * k:RW * k + b - a], src, "rel%d" % k, OFF)
+        write([server[Y, q] for Y in others if j or (Y, q, part) not in mrel], T.xw[:, a:b], src, "xin", OFF)
+
+    if isr:
+        gn("le")
+        write([server[Y, r] for Y in others], T.le[:], T.le[:], "lst", OFF)
+        for j in (0, 1):
+            a, b = PIECES[1][j]
+            gn("x1%d" % j)
+            write([relay[core]], T.rl[:, RW * j:RW * j + b - a], T.xw[:, a:b], "rel%d" % j, HI)
+        for j in (0, 1):
+            a, b = PIECES[0][j]
+            gn("x0%d" % j)
+            out_piece(r, 0, j, T.xw[:, a:b])
+    did(g.iota(T.colT[:], [[1, 256]], 1, 0, **row), "colT")
+    if isr:
+        did(g.iota(T.colH[:], [[1, 4], [0, 32]], EL * dloc, 0, **row), "colH")
+    for c in dests:
+        if relay[c] == core:
+            for j in (0, 1):
+                a, b = PIECES[1][j]
+                g.wait_ge(T.sem["rel%d" % j], bits(HI))
+                out_piece(cores.index(c), 1, j, T.rl[:, RW * j:RW * j + b - a])
+
+    S = lambda i, n=1: T.sc[:, i:i + n]
+    TH0, TH, PMG, EK, ISQ = 24, 28, 32, 40, 44
+    B30 = lambda s, n=1: T.tb[:, 30 * s:30 * s + 30 * n]
+    T6, T3, TA, TC, TD, TE, PG = 13, 19, 22, 23, 24, 25, 26
+    I8 = T.colX[:, 112:120]
+    vn("pi")
+    did(v.tensor_scalar(T.ia[:, 0:1], T.pi[:], 15, None, Op.bitwise_and), "ia")
+    did(v.tensor_scalar(T.ia[:, 1:2], T.pi[:], 4, None, Op.arith_shift_right), "ia")
+    did(v.tensor_scalar(T.ia[:, 2:3], T.pi[:], 0, None, Op.arith_shift_right), "ia")
+    if isr:
+        did(v.tensor_scalar(T.ia[:, 3:4], T.pi[:], 4, 1, Op.arith_shift_right, Op.bitwise_and), "ia")
+        did(v.tensor_scalar(T.ia[:, 4:5], T.pi[:], 5, None, Op.arith_shift_right), "ia")
+    vn("ia")
+    did(v.tensor_copy(S(0, 3), T.ia[:, 0:3]), "sc")
+    vn("sc", "colX", "colA", "colG")
+    did(v.tensor_scalar(S(PMG, 8), I8, -1.0, S(2), Op.mult, Op.add), "pmg")
+    did(v.tensor_scalar(S(EK, 4), T.colX[:, 112:144:8], S(1), None, Op.add), "ek")
+    vn("pmg")
+    for q in range(8):
+        did(v.tensor_scalar(T.rg[:, 128 * q:128 * q + 128], T.colA[:, 0:128], 8.0, S(PMG + q), Op.mult, Op.is_equal), "rg")
+    did(v.memset(T.ps[:], 0.0), "ps0")
+    if asks:
+        did(v.memset(T.ps2[:], 0.0), "ps20")
+    did(v.tensor_scalar(T.bo[:], T.colG[:], S(1), None, Op.is_equal), "bo")
+    did(v.tensor_scalar(T.gt[:], T.colA[:, 0:128], S(0), None, Op.is_gt), "gt")
+    vn("bo", "gt")
+    did(v.tensor_tensor(T.u1[:], T.bo[:], T.gt[:], Op.mult), "u1")
+    did(v.tensor_scalar(T.rep[:], T.colA[:, 0:128], S(0), None, Op.is_equal), "rep")
+
+    if isr:
+        vn("le")
+    else:
+        v.wait_ge(T.sem.lst, bits(OFF))
+    did(v.tensor_copy(T.lb[:], T.le[:]), "lb")
+    pn("lb", "rg")
+    for q in range(8):
+        did(pe.matmul(T.p0[:, 32 * q:32 * q + 32], T.rg[:, 128 * q:128 * q + 128], T.lb[:, 0:32], True, True), "E1")
+    if asks:
+        for q in range(8):
+            did(pe.matmul(T.p1[:, 32 * q:32 * q + 32], T.rg[:, 128 * q:128 * q + 128], T.lb[:, 32:64], True, True), "E2")
+    rounds = [x] + [i for i in range(4) if i != x]
+    ocol = lambda i: (256 * i, 256 * i + 256)
+    vn("E1", "ek")
+    for i in rounds:
+        a, b = ocol(i)
+        did(v.tensor_scalar(T.o1[:, a:b], T.p0[:, 0:256], S(EK + i), None, Op.is_equal), "o1_%d" % i)
+    vn("ps0")
+    for i in rounds:
+        a, b = ocol(i)
+        vn("o1_%d" % i)
+        did(v.tensor_tensor_scan(T.ps[:, PB * i + 8:PB * i + PB], T.o1[:, a:b], T.o1[:, a:b], 0.0, Op.add, Op.max), "ps")
+    vn("ps")
+    did(v.tensor_copy(T.cl[:], T.ps[:, PB - 1::PB]), "cl")
+
+    gn("cl")
+    lat = [server[X, q] for q in range(N) if q > r and (q >= FIRST2 or server[X, q] in dests)]
+    write(lat, T.ld1[:, 4 * r:4 * r + 4], T.cl[:], "c1a", cmask(core))
+    write([c for c in dests if cores.index(c) < r], T.ld1[:, 4 * r:4 * r + 4], T.cl[:], "c1b", cmask(core))
+    landed = lambda qs: sum(bits(cmask(server[X, q])) for q in qs)
+
+    bank = {}
+    pn("u1", "bo", "ps", *["o1_%d" % i for i in rounds])
+    use = rounds if asks else rounds[:1]
+    for j, i in enumerate(use):
+        a, b = ocol(i)
+        bank[i] = [T.p2, T.p3][j // 2][:, 256 * (j % 2):256 * (j % 2) + 256]
+        did(pe.matmul(bank[i], T.u1[:], T.o1[:, a:b], True, False), "W%d" % (j // 2))
+        did(pe.matmul(bank[i], T.bo[:], T.ps[:, PB * i + 7:PB * i + PB - 1], False, True), "W%d" % (j // 2))
+    did(v.tensor_scalar(S(8), S(1), 2.0, float(CAPP), Op.add, Op.mult), "sc8")
+    did(v.tensor_scalar(S(3), S(0), 0.0, None, Op.is_equal), "sc3")
+    did(v.tensor_scalar(S(4), S(0), 1.0, None, Op.is_equal), "sc4")
+    did(v.tensor_scalar(S(5), S(0), 2.0, None, Op.is_lt), "sc5")
+    did(v.tensor_scalar(T.wide[:], T.colX[:], S(0), None, Op.is_equal), "wide")
+    vn("sc8")
+    did(v.tensor_scalar(T.wideW[:], T.colX[:], S(0), S(8), Op.is_equal, Op.mult), "wide")
+    did(v.tensor_scalar(T.trash[:], T.colX[:, 112:144], 16.0, S(0), Op.mult, Op.add), "trash")
+    vn("sc4", "sc5")
+    did(v.tensor_scalar(S(6), S(1), float(NTOK8), S(4), Op.mult, Op.mult), "sc6")
+    did(v.tensor_scalar(T.wd[:], T.colA[:], 15.0, S(5), Op.is_equal, Op.mult), "wd")
+    vn("sc6")
+    did(v.tensor_scalar(S(7), S(4), 256.0, S(6), Op.mult, Op.add), "sc7")
+    did(v.memset(T.win1[:, NTOK8:], 0.0), "win1")
+
+    def mult1(i):
+        a, b = ocol(i)
+        did(v.tensor_tensor(T.m1[:, a:b], bank[i], T.o1[:, a:b], Op.mult), "m1_%d" % i)
+
+    vn("W0")
+    for i in use[:2]:
+        mult1(i)
+    vn("colT", "sc3", "sc7")
+    did(v.tensor_scalar(T.dat[:, 0:256], T.colT[:], S(3), S(6), Op.mult, Op.add), "dat")
+    did(v.tensor_scalar(T.dat[:, 256:512], T.colT[:], S(3), S(7), Op.mult, Op.add), "dat")
+    if asks:
+        vn("W1")
+        for i in use[2:]:
+            mult1(i)
+        vn("E2")
+        did(v.tensor_scalar(T.hh[:], T.p1[:, 0:256], S(EK + x), 1048576.0, Op.not_equal, Op.mult), "hh")
+
+    def targets(m, o, names, ps, key):
+        pn("wide", *names)
+        for q in range(8):
+            s = slice(32 * q, 32 * q + 32)
+            w = slice(112 - 16 * q, 240 - 16 * q)
+            did(pe.matmul(ps[:, 0:32], T.wide[:, w], m(s), q == 0, False), key)
+            did(pe.matmul(ps[:, 0:32], T.wideW[:, w], o(s), False, q == 7), key)
+
+    def scatter(ps, tf, to, win, tkey, wkey, key):
+        vn(tkey, "trash")
+        did(v.tensor_tensor(tf, ps[:, 0:32], T.trash[:], Op.max), key + "f")
+        vn(key + "f")
+        did(v.tensor_copy(to[:], tf), key + "o")
+        vn(key + "o", wkey, "dat")
+        did(v.tensor_copy(win[:, :].indirect(to[:, :]), T.dat[:]), key)
+
+    def merge(win, ps, off, key, mkey, okey):
+        pn("wd", key)
+        for a in range(16):
+            did(pe.matmul(ps[:, 0:SLOTS // 16], T.wd[:, 15 - a:143 - a], win[:, NTOK8 + a::16], a == 0, a == 15), mkey)
+        vn(mkey)
+        did(v.tensor_scalar(off[:], ps[:, 0:SLOTS // 16], -1.0, 0.0, Op.add, Op.max), okey)
+
+    a0 = 256 * x
+    targets(lambda s: T.m1[:, a0 + s.start:a0 + s.stop], lambda s: T.o1[:, a0 + s.start:a0 + s.stop], ["m1_%d" % x, "o1_%d" % x], T.p6, "tg1")
+    if asks:
+        pn("rep")
+        for j, i in enumerate(rounds):
+            a, b = ocol(i)
+            pn("m1_%d" % i)
+            did(pe.matmul(T.p4[:, 0:256], T.rep[:], T.m1[:, a:b], j == 0, False), "D")
+    scatter(T.p6, T.tf[:, 0:32], T.to1, T.win1, "tg1", "win1", "sc1")
+    if asks:
+        did(v.memset(T.win2[:, NTOK8:], 0.0), "win2")
+    merge(T.win1, T.p7, T.off1, "sc1", "mg1", "off1")
+
+    if asks:
+        before = [q for q in range(N) if q < r]
+        pe.wait_ge(T.sem.c1a, landed(before))
+        for q in before:
+            did(pe.matmul(T.p5[:, 0:4], T.bo[:], T.ld1[:, 4 * q:4 * q + 4], q == 0, q == before[-1]), "base")
+        vn("base")
+        did(v.tensor_scalar(S(TH0, 4), T.p5[:, 0:4], -float(CAP), 0.0, Op.add, Op.min), "th0")
+        vn("th0")
+        did(v.tensor_scalar(S(TH, 4), S(TH0, 4), -float(CAPP), None, Op.max), "th")
+        vn("th", "rep")
+        for i in rounds:
+            did(v.tensor_scalar(T.thr[:, 128 * i:128 * i + 128], T.rep[:], S(TH + i), None, Op.mult), "thr")
+        pn("thr")
+        for j, i in enumerate(rounds):
+            a, b = ocol(i)
+            did(pe.matmul(T.p4[:, 0:256], T.thr[:, 128 * i:128 * i + 128], T.o1[:, a:b], False, j == 3), "D")
+        vn("D", "hh")
+        did(v.tensor_tensor(T.o2[:], T.p4[:, 0:256], T.hh[:], Op.is_ge), "o2")
+        vn("o2", "ps20")
+        did(v.tensor_tensor_scan(T.ps2[:, 8:PB], T.o2[:], T.o2[:], 0.0, Op.add, Op.max), "ps2")
+        vn("ps2")
+        did(v.tensor_copy(T.cl2[:], T.ps2[:, PB - 2:PB]), "cl2")
+        gn("cl2")
+        write([c for c in dests if c != core], T.ld2[:, 2 * r:2 * r + 2], T.cl2[:], "c2", cmask(core))
+        pn("o2", "ps2")
+        did(pe.matmul(T.p0[:, 0:256], T.u1[:], T.o2[:], True, False), "W2")
+        did(pe.matmul(T.p0[:, 0:256], T.bo[:], T.ps2[:, 7:PB - 1], False, True), "W2")
+        vn("W2")
+        did(v.tensor_tensor(T.m2[:], T.p0[:, 0:256], T.o2[:], Op.mult), "m2")
+        targets(lambda s: T.m2[:, s], lambda s: T.o2[:, s], ["m2", "o2"], T.p1, "tg2")
+        scatter(T.p1, T.tf[:, 32:64], T.to2, T.win2, "tg2", "win2", "sc2")
+        merge(T.win2, T.p5, T.off2, "sc2", "mg2", "off2")
+
+    blocks = [(t, d) for t in ((0, 1) if asks else (0,)) for d in (0, 1)]
+    onvec = {b: (b == (1, 0)) if isr else b[1] == 0 for b in blocks}
+    slot = lambda t: (r if t == 0 else N + r - FIRST2) * BLK
+    pmask = lambda c: HI if c in dests else ON
+    for eng in (True, False):
+        q, k = (v, "v") if eng else (sa, "a")
+        todo = [b for b in blocks if onvec[b] == eng]
+        if todo and isr:
+            need(q, k, "x00", "x01", "x10", "x11")
+        elif todo:
+            q.wait_ge(T.sem.xin, 4 * bits(OFF))
+        for t, d in todo:
+            need(q, k, ("off1", "off2")[t])
+            src = T.xw[:, 0:NT].indirect((T.off1, T.off2)[t][:, 64 * d:64 * d + 64])
+            s, n = slot(t), (2 * t + d) * BLK
+            out = T.pk[:, s:s + BLK] if dests[d] == core else T.ob[:, n:n + BLK]
+            did(v.tensor_copy(out, src) if eng else sa.activation(out, src, Act.Copy), "pack%d%d" % (t, d))
+    for t, d in blocks:
+        if dests[d] != core:
+            s, n = slot(t), (2 * t + d) * BLK
+            gn("pack%d%d" % (t, d))
+            write([dests[d]], T.pk[:, s:s + BLK], T.ob[:, n:n + BLK], "pin", pmask(core))
+
+    if isr:
+        did(v.memset(T.pk[:, ZERO:], 0.0), "zero")
+        did(v.memset(T.cap[:], float(CAP)), "cap")
+        did(v.memset(T.bq[:, 0:1], 0.0), "bq0")
+        did(v.tensor_copy(S(11), T.ia[:, 3:4]), "sc11")
+        did(v.tensor_scalar(S(10), T.ia[:, 4:5], float(CAPP), None, Op.mult), "sc10")
+        vn("sc11", "colH")
+        did(v.tensor_scalar(S(9), S(11), float(CAP // 2), S(0), Op.mult, Op.add), "sc9")
+        did(v.tensor_scalar(T.mapd[:], T.colH[:], S(1), None, Op.is_equal), "mapd")
+        did(v.tensor_scalar(S(ISQ, 8), I8, S(1), None, Op.is_equal), "isq")
+        vn("sc9", "sc10", "isq", "rep")
+        did(v.tensor_scalar(B30(PG), T.colX[:, 112:142], 16.0, S(9), Op.mult, Op.add), "pg")
+        for q in range(8):
+            did(v.tensor_scalar(T.repq[:, 128 * q:128 * q + 128], T.rep[:], S(ISQ + q), None, Op.mult), "repq")
+        if r and not asks:
+            pe.wait_ge(T.sem.c1a, landed(range(r)))
+        if r < N - 1:
+            pe.wait_ge(T.sem.c1b, landed(range(r + 1, N)))
+        pe.wait_ge(T.sem.c2, landed(q for q in range(FIRST2, N) if q != r))
+        pn("mapd", "cl", *(["m1_%d" % i for i in use] + (["cl2"] if asks else [])))
+        for q in range(N):
+            src = T.cl[:, x:x + 1] if q == r else T.ld1[:, 4 * q + x:4 * q + x + 1]
+            did(pe.matmul(T.p2[:, q:q + 1], T.mapd[:], src, True, True), "ns")
+        for q in range(FIRST2, N):
+            src = T.cl2[:, 1:2] if q == r else T.ld2[:, 2 * q + 1:2 * q + 2]
+            did(pe.matmul(T.p2[:, N + q - FIRST2:N + q - FIRST2 + 1], T.mapd[:], src, True, True), "ns")
+        vn("ns", "cap", "bq0")
+        did(v.tensor_tensor_scan(T.bq[:, 1:NSEG + 1], T.p2[:, 0:NSEG], T.cap[:], 0.0, Op.add, Op.min), "bq")
+        vn("bq")
+        did(v.tensor_tensor(T.db[:], T.bq[:, 1:NSEG + 1], T.bq[:, 0:NSEG], Op.subtract), "db")
+        vn("db")
+        L = NSEG - 1
+        did(v.tensor_scalar(T.dl[:, 0:L], T.db[:, 0:L], -1.0, float(BLK), Op.mult, Op.add), "dl")
+        did(v.tensor_scalar(S(12), T.db[:, L:L + 1], -1.0, float(BLK), Op.mult, Op.add), "td0")
+        vn("td0")
+        did(v.tensor_scalar(T.dl[:, L:L + 1], S(12), S(10), None, Op.subtract), "dl")
+        vn("dl", "pg")
+        for s in range(NSEG):
+            did(v.tensor_scalar(B30(s), B30(PG), T.bq[:, s + 1:s + 2], T.dl[:, s:s + 1], Op.is_ge, Op.mult), "tb")
+        did(v.tensor_scalar(B30(TA), B30(PG), S(10), None, Op.add), "ta")
+        vn("tb", "ta")
+        did(v.tensor_tensor(B30(T6, 6), B30(0, 6), B30(6, 6), Op.add), "t6")
+        did(v.tensor_tensor(B30(TC), B30(TA), B30(12), Op.add), "tc")
+        vn("t6")
+        did(v.tensor_tensor(B30(T3, 3), B30(T6, 3), B30(T6 + 3, 3), Op.add), "t3")
+        vn("t3", "tc")
+        did(v.tensor_tensor(B30(TD), B30(T3), B30(T3 + 1), Op.add), "td")
+        did(v.tensor_tensor(B30(TE), B30(T3 + 2), B30(TC), Op.add), "te")
+        vn("td", "te")
+        did(v.tensor_tensor(B30(TA), B30(TD), B30(TE), Op.add), "src")
+        vn("src")
+        did(v.tensor_copy(T.hl[:, 0:30], B30(TA)), "hb")
+        vn("hb")
+        did(v.tensor_tensor(T.hl[:, 30:60], B30(TA), T.hl[:, 0:30], Op.subtract), "lo")
+        pn("hb", "lo", "repq")
+        for q in range(8):
+            for i in (0, 1):
+                did(pe.matmul(T.p3[:, 30 * q:30 * q + 30], T.repq[:, 128 * q:128 * q + 128], T.hl[:, 30 * i:30 * i + 30], i == 0, i == 1), "of")
+        vn("of")
+        did(v.tensor_copy(T.offF[:], T.p3[:, 0:240]), "offF")
+        inn = sum(bits(pmask(server[X, q])) * (2 if q >= FIRST2 else 1) for q in range(N) if q != r)
+        mine = ["pack%d%d" % b for b in blocks if dests[b[1]] == core]
+        for q, k, ks in ((v, "v", (0, 1)), (sa, "a", (2, 3))):
+            need(q, k, "offF", "zero", *mine)
+            q.wait_ge(T.sem.pin, inn)
+            for kk in ks:
+                src = T.pk[:, :].indirect(T.offF[:, 60 * kk:60 * kk + 60])
+                out = T.ys[:, CAP * kk:CAP * kk + CAP]
+                did(v.tensor_copy(out, src) if k == "v" else sa.activation(out, src, Act.Copy), "ys%d" % kk)
+        for kk in (0, 2, 1, 3):
+            need(sy, "y", "ys%d" % kk)
+            did(sy.dma_start(T.y[:, CAP * kk:CAP * kk + CAP], T.ys[:, CAP * kk:CAP * kk + CAP]), "y", 16)
+        need(sy, "y", "y")
+    g.wait_ge(T.sem.sent, sent[0])
+    gn(*[nm for nm in num if not [k for k, m in seen if m == nm and seen[k, m] == cnt[nm]]])

@@ -3,11 +3,13 @@ from concourse.mybir import AluOpType as Op, ActivationFunctionType as Act
 
 NC, N, NT, EL, CAP, CAPP = 128, 8, 4096, 4, 960, 256
 FIRST2 = CAP // CAPP
-BLK = EL * CAPP
 NSEG = N + N - FIRST2
-ZERO = NSEG * BLK
-PIECES = [[(0, 1088), (1088, 2176)], [(2176, 3136), (3136, 4096)]]
-RW = 1088
+HB = EL // 2 * CAPP
+pos = lambda q: HB * q + HB * max(0, q - FIRST2)
+ZERO = HB * NSEG
+PIECES = [[(0, 1184), (1184, 2240)], [(2240, 3216), (3216, 4096)]]
+WHOLE = [(0, 2240), (2240, 4096)]
+R0, RW = 2240, 1184
 PB = 264
 NTOK8, SLOTS = NT // 8, 8 * CAPP
 
@@ -15,17 +17,18 @@ SCRATCH = {"p%d" % _i: ("psum", [128, 512], "float32") for _i in range(8)}
 for _d, _b in (
     ("bfloat16", dict(
         xw=NT, rl=2 * RW,
-        pk=ZERO + CAP, ys=EL * CAP, ob=4 * BLK,
+        pk0=ZERO + CAP, pk1=ZERO + CAP,
+        ys=EL * CAP, ob=8 * HB,
         cl=4, ld1=4 * N, cl2=2, ld2=2 * N,
         colA=144, colG=128, colX=240, colT=256, colH=128, rg=1024, bo=128, rep=128, gt=128, u1=128, wd=144, wide=240, wideW=240,
         mapd=128, repq=1024, dat=NTOK8, lb=64, o1=1024, m1=1024, ps=4 * PB, ps2=PB, hh=256, o2=256, m2=256, thr=512,
         win1=NTOK8 + SLOTS, win2=NTOK8 + SLOTS, hl=60)),
-    ("float32", dict(sc=64, trash=32, tf=64, cap=NSEG, bq=NSEG + 1, db=NSEG, dl=NSEG, tb=30 * NSEG + 420)),
+    ("float32", dict(sc=64, trash=32, tf=64, cap=2 * NSEG, bq=NSEG + 1, db=NSEG, dl=NSEG, tb=30 * NSEG + 420)),
     ("int32", dict(le=64, pi=1, ia=8)),
     ("uint16", dict(to1=32, to2=32, off1=SLOTS // 16, off2=SLOTS // 16, offF=EL * CAP // 16)),
 ):
     SCRATCH.update({_n: ("sbuf", [128, _w], _d) for _n, _w in _b.items()})
-SEMAPHORES = ["lst", "xin", "c1a", "c1b", "c2", "pin", "rel0", "rel1", "sent"] + ["s%d" % i for i in range(130)]
+SEMAPHORES = ["lst", "xin", "c1a", "c1b", "c2", "pin0", "pin1", "rel0", "rel1", "sent"] + ["s%d" % i for i in range(140)]
 
 
 def plan(T, topo):
@@ -40,12 +43,12 @@ def plan(T, topo):
     server, relay, mrel = {}, {}, {}
     for X in chips:
         own = [c for c in cores if topo.chip(c) == X]
-        free = [c for c in on[X] if c not in own]
-        for r, c in enumerate(cores):
-            server[X, r] = c if c in own else free.pop(0)
         cand = [c for c in on[X] if topo.die(c) != topo.die(own[0]) and all(topo.may_write(c, d) for d in cores if topo.chip(d) != X)]
         for i, c in enumerate(own):
             relay[c] = cand[i]
+        free = sorted((c for c in on[X] if c not in own), key=lambda c: (topo.die(c) != topo.die(own[0]), c in cand))
+        for r in sorted(range(N), key=lambda q: (not topo.same_plane(X, topo.chip(cores[q])), q)):
+            server[X, r] = cores[r] if cores[r] in own else free.pop(0)
     for X in chips:
         M = [m for m in on if topo.mates(X, m)][0]
         far = [A for A in chips if A != X and not topo.same_plane(A, X)]
@@ -115,11 +118,10 @@ def rank_program(g, core, T, topo):
     def pn(*a): need(pe, "p", *a)
     def gn(*a): need(g, "g", *a)
 
-    flat = [(1, 0), (1, 1), (0, 0), (0, 1)]
     if isr:
         did(sy.dma_start(T.le[:, 0:32], T.e1[:]), "le", 16)
         did(sa.dma_start(T.le[:, 32:64], T.e2[:]), "le", 16)
-        for i, (p, j) in enumerate(flat):
+        for i, (p, j) in enumerate([(1, 0), (1, 1), (0, 0), (0, 1)]):
             a, b = PIECES[p][j]
             did((sy if i % 2 == 0 else sa).dma_start(T.xw[:, a:b], T.x[:, a:b]), "x%d%d" % (p, j), 16)
 
@@ -128,35 +130,40 @@ def rank_program(g, core, T, topo):
     did(g.iota(T.colX[:], [[1, 240]], -112, 0, **row), "colX")
     did(g.iota(T.colA[:], [[0, 9], [1, 16]], 0, 0, **row), "colA")
     did(g.iota(T.colG[:], [[1, 8], [0, 16]], 0, 0, **row), "colG")
+    did(g.iota(T.colT[:], [[1, 256]], 1, 0, **row), "colT")
 
-    def out_piece(q, part, j, src):
-        a, b = PIECES[part][j]
-        via = [mrel[Y, q, part] for Y in others if (Y, q, part) in mrel] if j == 0 else []
-        if via:
-            k = via[0][1]
-            write([m[0] for m in via], T.rl[:, RW * k:RW * k + b - a], src, "rel%d" % k, OFF)
-        write([server[Y, q] for Y in others if j or (Y, q, part) not in mrel], T.xw[:, a:b], src, "xin", OFF)
+    def by_mates(q, part, src):
+        via = [mrel[Y, q, part] for Y in others if (Y, q, part) in mrel]
+        a, b = PIECES[part][0]
+        k = via[0][1]
+        write([m[0] for m in via], T.rl[:, RW * k:RW * k + b - a], src, "rel%d" % k, OFF)
 
+    def direct(q, part, src):
+        a, b = PIECES[part][1]
+        write([server[Y, q] for Y in others if (Y, q, part) in mrel], T.xw[:, a:b], src, "xin", OFF)
+
+    def in_plane(q, part, src):
+        a, b = WHOLE[part]
+        write([server[Y, q] for Y in others if (Y, q, part) not in mrel], T.xw[:, a:b], src, "xin", OFF)
+
+    X_ = lambda ab: T.xw[:, ab[0]:ab[1]]
+    R_ = lambda ab: T.rl[:, ab[0] - R0:ab[1] - R0]
     if isr:
         gn("le")
         write([server[Y, r] for Y in others], T.le[:], T.le[:], "lst", OFF)
         for j in (0, 1):
-            a, b = PIECES[1][j]
             gn("x1%d" % j)
-            write([relay[core]], T.rl[:, RW * j:RW * j + b - a], T.xw[:, a:b], "rel%d" % j, HI)
-        for j in (0, 1):
-            a, b = PIECES[0][j]
-            gn("x0%d" % j)
-            out_piece(r, 0, j, T.xw[:, a:b])
-    did(g.iota(T.colT[:], [[1, 256]], 1, 0, **row), "colT")
-    if isr:
+            write([relay[core]], R_(PIECES[1][j]), X_(PIECES[1][j]), "rel%d" % j, HI)
+        gn("x00")
+        by_mates(r, 0, X_(PIECES[0][0]))
+        gn("x01")
+        direct(r, 0, X_(PIECES[0][1]))
+        in_plane(r, 0, X_(WHOLE[0]))
         did(g.iota(T.colH[:], [[1, 4], [0, 32]], EL * dloc, 0, **row), "colH")
-    for c in dests:
-        if relay[c] == core:
-            for j in (0, 1):
-                a, b = PIECES[1][j]
-                g.wait_ge(T.sem["rel%d" % j], bits(HI))
-                out_piece(cores.index(c), 1, j, T.rl[:, RW * j:RW * j + b - a])
+    passes = [cores.index(c) for c in dests if relay[c] == core]
+    if passes:
+        g.wait_ge(T.sem.rel0, bits(HI))
+        by_mates(passes[0], 1, R_(PIECES[1][0]))
 
     S = lambda i, n=1: T.sc[:, i:i + n]
     TH0, TH, PMG, EK, ISQ = 24, 28, 32, 40, 44
@@ -169,7 +176,7 @@ def rank_program(g, core, T, topo):
     did(v.tensor_scalar(T.ia[:, 2:3], T.pi[:], 0, None, Op.arith_shift_right), "ia")
     if isr:
         did(v.tensor_scalar(T.ia[:, 3:4], T.pi[:], 4, 1, Op.arith_shift_right, Op.bitwise_and), "ia")
-        did(v.tensor_scalar(T.ia[:, 4:5], T.pi[:], 5, None, Op.arith_shift_right), "ia")
+        did(v.tensor_scalar(T.ia[:, 4:5], T.pi[:], 5, 1, Op.arith_shift_right, Op.bitwise_and), "ia")
     vn("ia")
     did(v.tensor_copy(S(0, 3), T.ia[:, 0:3]), "sc")
     vn("sc", "colX", "colA", "colG")
@@ -183,9 +190,26 @@ def rank_program(g, core, T, topo):
         did(v.memset(T.ps2[:], 0.0), "ps20")
     did(v.tensor_scalar(T.bo[:], T.colG[:], S(1), None, Op.is_equal), "bo")
     did(v.tensor_scalar(T.gt[:], T.colA[:, 0:128], S(0), None, Op.is_gt), "gt")
+    did(v.tensor_scalar(T.rep[:], T.colA[:, 0:128], S(0), None, Op.is_equal), "rep")
     vn("bo", "gt")
     did(v.tensor_tensor(T.u1[:], T.bo[:], T.gt[:], Op.mult), "u1")
-    did(v.tensor_scalar(T.rep[:], T.colA[:, 0:128], S(0), None, Op.is_equal), "rep")
+    did(v.tensor_scalar(S(8), S(1), 2.0, float(CAPP), Op.add, Op.mult), "sc8")
+    did(v.tensor_scalar(S(3), S(0), 0.0, None, Op.is_equal), "sc3")
+    did(v.tensor_scalar(S(4), S(0), 1.0, None, Op.is_equal), "sc4")
+    did(v.tensor_scalar(S(5), S(0), 2.0, None, Op.is_lt), "sc5")
+    did(v.tensor_scalar(T.wide[:], T.colX[:], S(0), None, Op.is_equal), "wide")
+    vn("sc8")
+    did(v.tensor_scalar(T.wideW[:], T.colX[:], S(0), S(8), Op.is_equal, Op.mult), "wide")
+    did(v.tensor_scalar(T.trash[:], T.colX[:, 112:144], 16.0, S(0), Op.mult, Op.add), "trash")
+    vn("sc4", "sc5")
+    did(v.tensor_scalar(S(6), S(1), float(NTOK8), S(4), Op.mult, Op.mult), "sc6")
+    did(v.tensor_scalar(T.wd[:], T.colA[:], 15.0, S(5), Op.is_equal, Op.mult), "wd")
+    vn("sc6")
+    did(v.tensor_scalar(S(7), S(4), 256.0, S(6), Op.mult, Op.add), "sc7")
+    vn("colT", "sc3", "sc7")
+    did(v.tensor_scalar(T.dat[:, 0:256], T.colT[:], S(3), S(6), Op.mult, Op.add), "dat")
+    did(v.tensor_scalar(T.dat[:, 256:512], T.colT[:], S(3), S(7), Op.mult, Op.add), "dat")
+    did(v.memset(T.win1[:, NTOK8:], 0.0), "win1")
 
     if isr:
         vn("le")
@@ -208,8 +232,8 @@ def rank_program(g, core, T, topo):
     for i in rounds:
         a, b = ocol(i)
         vn("o1_%d" % i)
-        did(v.tensor_tensor_scan(T.ps[:, PB * i + 8:PB * i + PB], T.o1[:, a:b], T.o1[:, a:b], 0.0, Op.add, Op.max), "ps")
-    vn("ps")
+        did(v.tensor_tensor_scan(T.ps[:, PB * i + 8:PB * i + PB], T.o1[:, a:b], T.o1[:, a:b], 0.0, Op.add, Op.max), "ps_%d" % i)
+    vn(*["ps_%d" % i for i in rounds])
     did(v.tensor_copy(T.cl[:], T.ps[:, PB - 1::PB]), "cl")
 
     gn("cl")
@@ -217,46 +241,30 @@ def rank_program(g, core, T, topo):
     write(lat, T.ld1[:, 4 * r:4 * r + 4], T.cl[:], "c1a", cmask(core))
     write([c for c in dests if cores.index(c) < r], T.ld1[:, 4 * r:4 * r + 4], T.cl[:], "c1b", cmask(core))
     landed = lambda qs: sum(bits(cmask(server[X, q])) for q in qs)
+    if passes:
+        g.wait_ge(T.sem.rel1, bits(HI))
+        direct(passes[0], 1, R_(PIECES[1][1]))
+        in_plane(passes[0], 1, R_(WHOLE[1]))
 
     bank = {}
-    pn("u1", "bo", "ps", *["o1_%d" % i for i in rounds])
+    pn("u1", "bo")
     use = rounds if asks else rounds[:1]
     for j, i in enumerate(use):
         a, b = ocol(i)
         bank[i] = [T.p2, T.p3][j // 2][:, 256 * (j % 2):256 * (j % 2) + 256]
+        pn("o1_%d" % i)
         did(pe.matmul(bank[i], T.u1[:], T.o1[:, a:b], True, False), "W%d" % (j // 2))
+        pn("ps_%d" % i)
         did(pe.matmul(bank[i], T.bo[:], T.ps[:, PB * i + 7:PB * i + PB - 1], False, True), "W%d" % (j // 2))
-    did(v.tensor_scalar(S(8), S(1), 2.0, float(CAPP), Op.add, Op.mult), "sc8")
-    did(v.tensor_scalar(S(3), S(0), 0.0, None, Op.is_equal), "sc3")
-    did(v.tensor_scalar(S(4), S(0), 1.0, None, Op.is_equal), "sc4")
-    did(v.tensor_scalar(S(5), S(0), 2.0, None, Op.is_lt), "sc5")
-    did(v.tensor_scalar(T.wide[:], T.colX[:], S(0), None, Op.is_equal), "wide")
-    vn("sc8")
-    did(v.tensor_scalar(T.wideW[:], T.colX[:], S(0), S(8), Op.is_equal, Op.mult), "wide")
-    did(v.tensor_scalar(T.trash[:], T.colX[:, 112:144], 16.0, S(0), Op.mult, Op.add), "trash")
-    vn("sc4", "sc5")
-    did(v.tensor_scalar(S(6), S(1), float(NTOK8), S(4), Op.mult, Op.mult), "sc6")
-    did(v.tensor_scalar(T.wd[:], T.colA[:], 15.0, S(5), Op.is_equal, Op.mult), "wd")
-    vn("sc6")
-    did(v.tensor_scalar(S(7), S(4), 256.0, S(6), Op.mult, Op.add), "sc7")
-    did(v.memset(T.win1[:, NTOK8:], 0.0), "win1")
-
-    def mult1(i):
-        a, b = ocol(i)
-        did(v.tensor_tensor(T.m1[:, a:b], bank[i], T.o1[:, a:b], Op.mult), "m1_%d" % i)
-
-    vn("W0")
-    for i in use[:2]:
-        mult1(i)
-    vn("colT", "sc3", "sc7")
-    did(v.tensor_scalar(T.dat[:, 0:256], T.colT[:], S(3), S(6), Op.mult, Op.add), "dat")
-    did(v.tensor_scalar(T.dat[:, 256:512], T.colT[:], S(3), S(7), Op.mult, Op.add), "dat")
     if asks:
-        vn("W1")
-        for i in use[2:]:
-            mult1(i)
         vn("E2")
         did(v.tensor_scalar(T.hh[:], T.p1[:, 0:256], S(EK + x), 1048576.0, Op.not_equal, Op.mult), "hh")
+    for j, i in enumerate(use):
+        a, b = ocol(i)
+        vn("W%d" % (j // 2))
+        did(v.tensor_tensor(T.m1[:, a:b], bank[i], T.o1[:, a:b], Op.mult), "m1_%d" % i)
+    if asks:
+        did(v.memset(T.win2[:, NTOK8:], 0.0), "win2")
 
     def targets(m, o, names, ps, key):
         pn("wide", *names)
@@ -274,85 +282,51 @@ def rank_program(g, core, T, topo):
         vn(key + "o", wkey, "dat")
         did(v.tensor_copy(win[:, :].indirect(to[:, :]), T.dat[:]), key)
 
-    def merge(win, ps, off, key, mkey, okey):
+    def merge(win, ps, key, mkey):
         pn("wd", key)
         for a in range(16):
             did(pe.matmul(ps[:, 0:SLOTS // 16], T.wd[:, 15 - a:143 - a], win[:, NTOK8 + a::16], a == 0, a == 15), mkey)
+
+    def offsets(ps, off, mkey, okey):
         vn(mkey)
         did(v.tensor_scalar(off[:], ps[:, 0:SLOTS // 16], -1.0, 0.0, Op.add, Op.max), okey)
 
-    a0 = 256 * x
-    targets(lambda s: T.m1[:, a0 + s.start:a0 + s.stop], lambda s: T.o1[:, a0 + s.start:a0 + s.stop], ["m1_%d" % x, "o1_%d" % x], T.p6, "tg1")
-    if asks:
-        pn("rep")
-        for j, i in enumerate(rounds):
-            a, b = ocol(i)
-            pn("m1_%d" % i)
-            did(pe.matmul(T.p4[:, 0:256], T.rep[:], T.m1[:, a:b], j == 0, False), "D")
-    scatter(T.p6, T.tf[:, 0:32], T.to1, T.win1, "tg1", "win1", "sc1")
-    if asks:
-        did(v.memset(T.win2[:, NTOK8:], 0.0), "win2")
-    merge(T.win1, T.p7, T.off1, "sc1", "mg1", "off1")
+    def first_lists():
+        a0 = 256 * x
+        targets(lambda s: T.m1[:, a0 + s.start:a0 + s.stop], lambda s: T.o1[:, a0 + s.start:a0 + s.stop], ["m1_%d" % x, "o1_%d" % x], T.p6, "tg1")
+        scatter(T.p6, T.tf[:, 0:32], T.to1, T.win1, "tg1", "win1", "sc1")
 
-    if asks:
-        before = [q for q in range(N) if q < r]
-        pe.wait_ge(T.sem.c1a, landed(before))
-        for q in before:
-            did(pe.matmul(T.p5[:, 0:4], T.bo[:], T.ld1[:, 4 * q:4 * q + 4], q == 0, q == before[-1]), "base")
-        vn("base")
-        did(v.tensor_scalar(S(TH0, 4), T.p5[:, 0:4], -float(CAP), 0.0, Op.add, Op.min), "th0")
-        vn("th0")
-        did(v.tensor_scalar(S(TH, 4), S(TH0, 4), -float(CAPP), None, Op.max), "th")
-        vn("th", "rep")
-        for i in rounds:
-            did(v.tensor_scalar(T.thr[:, 128 * i:128 * i + 128], T.rep[:], S(TH + i), None, Op.mult), "thr")
-        pn("thr")
-        for j, i in enumerate(rounds):
-            a, b = ocol(i)
-            did(pe.matmul(T.p4[:, 0:256], T.thr[:, 128 * i:128 * i + 128], T.o1[:, a:b], False, j == 3), "D")
-        vn("D", "hh")
-        did(v.tensor_tensor(T.o2[:], T.p4[:, 0:256], T.hh[:], Op.is_ge), "o2")
-        vn("o2", "ps20")
-        did(v.tensor_tensor_scan(T.ps2[:, 8:PB], T.o2[:], T.o2[:], 0.0, Op.add, Op.max), "ps2")
-        vn("ps2")
-        did(v.tensor_copy(T.cl2[:], T.ps2[:, PB - 2:PB]), "cl2")
-        gn("cl2")
-        write([c for c in dests if c != core], T.ld2[:, 2 * r:2 * r + 2], T.cl2[:], "c2", cmask(core))
-        pn("o2", "ps2")
-        did(pe.matmul(T.p0[:, 0:256], T.u1[:], T.o2[:], True, False), "W2")
-        did(pe.matmul(T.p0[:, 0:256], T.bo[:], T.ps2[:, 7:PB - 1], False, True), "W2")
-        vn("W2")
-        did(v.tensor_tensor(T.m2[:], T.p0[:, 0:256], T.o2[:], Op.mult), "m2")
-        targets(lambda s: T.m2[:, s], lambda s: T.o2[:, s], ["m2", "o2"], T.p1, "tg2")
-        scatter(T.p1, T.tf[:, 32:64], T.to2, T.win2, "tg2", "win2", "sc2")
-        merge(T.win2, T.p5, T.off2, "sc2", "mg2", "off2")
-
-    blocks = [(t, d) for t in ((0, 1) if asks else (0,)) for d in (0, 1)]
-    onvec = {b: (b == (1, 0)) if isr else b[1] == 0 for b in blocks}
-    slot = lambda t: (r if t == 0 else N + r - FIRST2) * BLK
+    PK = (T.pk0, T.pk1)
+    width = (2 if asks else 1) * HB
+    calls = [(h, t, d) for h in (0, 1) for t in ((0, 1) if asks else (0,)) for d in (0, 1)]
     pmask = lambda c: HI if c in dests else ON
-    for eng in (True, False):
-        q, k = (v, "v") if eng else (sa, "a")
-        todo = [b for b in blocks if onvec[b] == eng]
+
+    def pack(q, k, todo):
         if todo and isr:
             need(q, k, "x00", "x01", "x10", "x11")
         elif todo:
-            q.wait_ge(T.sem.xin, 4 * bits(OFF))
-        for t, d in todo:
+            q.wait_ge(T.sem.xin, bits(OFF) * (2 if topo.same_plane(X, topo.chip(cores[r])) else 4))
+        for h, t, d in todo:
             need(q, k, ("off1", "off2")[t])
-            src = T.xw[:, 0:NT].indirect((T.off1, T.off2)[t][:, 64 * d:64 * d + 64])
-            s, n = slot(t), (2 * t + d) * BLK
-            out = T.pk[:, s:s + BLK] if dests[d] == core else T.ob[:, n:n + BLK]
-            did(v.tensor_copy(out, src) if eng else sa.activation(out, src, Act.Copy), "pack%d%d" % (t, d))
-    for t, d in blocks:
-        if dests[d] != core:
-            s, n = slot(t), (2 * t + d) * BLK
-            gn("pack%d%d" % (t, d))
-            write([dests[d]], T.pk[:, s:s + BLK], T.ob[:, n:n + BLK], "pin", pmask(core))
+            o = 64 * d + 32 * h
+            src = T.xw[:, 0:NT].indirect((T.off1, T.off2)[t][:, o:o + HB // 16])
+            s = HB * t + (pos(r) if dests[d] == core else 2 * HB * (2 * h + d))
+            out = (PK[h] if dests[d] == core else T.ob)[:, s:s + HB]
+            did(v.tensor_copy(out, src) if k == "v" else sa.activation(out, src, Act.Copy), "pack%d%d" % (h, d))
 
-    if isr:
-        did(v.memset(T.pk[:, ZERO:], 0.0), "zero")
-        did(v.memset(T.cap[:], float(CAP)), "cap")
+    def list_constants():
+        did(v.memset(T.pk0[:, ZERO:], 0.0), "zero")
+        did(v.memset(T.pk1[:, ZERO:], 0.0), "zero")
+        did(v.memset(T.cap[:, 0:NSEG], float(CAP)), "cap")
+        first = [pos(q) for q in range(N)] + [pos(q) + HB for q in range(FIRST2, N)] + [ZERO]
+        step = [first[s + 1] - first[s] for s in range(NSEG)]
+        s = 0
+        while s < NSEG:
+            e = s
+            while e < NSEG and step[e] == step[s]:
+                e += 1
+            did(v.memset(T.cap[:, NSEG + s:NSEG + e], float(step[s])), "cap")
+            s = e
         did(v.memset(T.bq[:, 0:1], 0.0), "bq0")
         did(v.tensor_copy(S(11), T.ia[:, 3:4]), "sc11")
         did(v.tensor_scalar(S(10), T.ia[:, 4:5], float(CAPP), None, Op.mult), "sc10")
@@ -364,6 +338,8 @@ def rank_program(g, core, T, topo):
         did(v.tensor_scalar(B30(PG), T.colX[:, 112:142], 16.0, S(9), Op.mult, Op.add), "pg")
         for q in range(8):
             did(v.tensor_scalar(T.repq[:, 128 * q:128 * q + 128], T.rep[:], S(ISQ + q), None, Op.mult), "repq")
+
+    def last_list():
         if r and not asks:
             pe.wait_ge(T.sem.c1a, landed(range(r)))
         if r < N - 1:
@@ -377,18 +353,17 @@ def rank_program(g, core, T, topo):
             src = T.cl2[:, 1:2] if q == r else T.ld2[:, 2 * q + 1:2 * q + 2]
             did(pe.matmul(T.p2[:, N + q - FIRST2:N + q - FIRST2 + 1], T.mapd[:], src, True, True), "ns")
         vn("ns", "cap", "bq0")
-        did(v.tensor_tensor_scan(T.bq[:, 1:NSEG + 1], T.p2[:, 0:NSEG], T.cap[:], 0.0, Op.add, Op.min), "bq")
+        did(v.tensor_tensor_scan(T.bq[:, 1:NSEG + 1], T.p2[:, 0:NSEG], T.cap[:, 0:NSEG], 0.0, Op.add, Op.min), "bq")
         vn("bq")
         did(v.tensor_tensor(T.db[:], T.bq[:, 1:NSEG + 1], T.bq[:, 0:NSEG], Op.subtract), "db")
         vn("db")
+        did(v.tensor_tensor(T.dl[:], T.cap[:, NSEG:2 * NSEG], T.db[:], Op.subtract), "dl")
+        vn("dl")
         L = NSEG - 1
-        did(v.tensor_scalar(T.dl[:, 0:L], T.db[:, 0:L], -1.0, float(BLK), Op.mult, Op.add), "dl")
-        did(v.tensor_scalar(S(12), T.db[:, L:L + 1], -1.0, float(BLK), Op.mult, Op.add), "td0")
-        vn("td0")
-        did(v.tensor_scalar(T.dl[:, L:L + 1], S(12), S(10), None, Op.subtract), "dl")
-        vn("dl", "pg")
+        did(v.tensor_scalar(S(12), T.dl[:, L:L + 1], S(10), None, Op.subtract), "dz")
+        vn("dz", "pg")
         for s in range(NSEG):
-            did(v.tensor_scalar(B30(s), B30(PG), T.bq[:, s + 1:s + 2], T.dl[:, s:s + 1], Op.is_ge, Op.mult), "tb")
+            did(v.tensor_scalar(B30(s), B30(PG), T.bq[:, s + 1:s + 2], T.dl[:, s:s + 1] if s < L else S(12), Op.is_ge, Op.mult), "tb")
         did(v.tensor_scalar(B30(TA), B30(PG), S(10), None, Op.add), "ta")
         vn("tb", "ta")
         did(v.tensor_tensor(B30(T6, 6), B30(0, 6), B30(6, 6), Op.add), "t6")
@@ -410,16 +385,85 @@ def rank_program(g, core, T, topo):
                 did(pe.matmul(T.p3[:, 30 * q:30 * q + 30], T.repq[:, 128 * q:128 * q + 128], T.hl[:, 30 * i:30 * i + 30], i == 0, i == 1), "of")
         vn("of")
         did(v.tensor_copy(T.offF[:], T.p3[:, 0:240]), "offF")
-        inn = sum(bits(pmask(server[X, q])) * (2 if q >= FIRST2 else 1) for q in range(N) if q != r)
-        mine = ["pack%d%d" % b for b in blocks if dests[b[1]] == core]
-        for q, k, ks in ((v, "v", (0, 1)), (sa, "a", (2, 3))):
-            need(q, k, "offF", "zero", *mine)
-            q.wait_ge(T.sem.pin, inn)
-            for kk in ks:
-                src = T.pk[:, :].indirect(T.offF[:, 60 * kk:60 * kk + 60])
-                out = T.ys[:, CAP * kk:CAP * kk + CAP]
-                did(v.tensor_copy(out, src) if k == "v" else sa.activation(out, src, Act.Copy), "ys%d" % kk)
-        for kk in (0, 2, 1, 3):
+
+    if asks:
+        pn("rep")
+        for j, i in enumerate(rounds):
+            a, b = ocol(i)
+            pn("m1_%d" % i)
+            did(pe.matmul(T.p4[:, 0:256], T.rep[:], T.m1[:, a:b], j == 0, False), "D")
+        first_lists()
+        if isr:
+            list_constants()
+        before = [q for q in range(N) if q < r]
+        pe.wait_ge(T.sem.c1a, landed(before))
+        for q in before:
+            did(pe.matmul(T.p5[:, 0:4], T.bo[:], T.ld1[:, 4 * q:4 * q + 4], q == 0, q == before[-1]), "base")
+        vn("base")
+        did(v.tensor_scalar(S(TH0, 4), T.p5[:, 0:4], -float(CAP), 0.0, Op.add, Op.min), "th0")
+        vn("th0")
+        did(v.tensor_scalar(S(TH, 4), S(TH0, 4), -float(CAPP), None, Op.max), "th")
+        vn("th", "rep")
+        for i in rounds:
+            did(v.tensor_scalar(T.thr[:, 128 * i:128 * i + 128], T.rep[:], S(TH + i), None, Op.mult), "thr%d" % i)
+        for j, i in enumerate(rounds):
+            a, b = ocol(i)
+            pn("thr%d" % i)
+            did(pe.matmul(T.p4[:, 0:256], T.thr[:, 128 * i:128 * i + 128], T.o1[:, a:b], False, j == 3), "D")
+        vn("D", "hh")
+        did(v.tensor_tensor(T.o2[:], T.p4[:, 0:256], T.hh[:], Op.is_ge), "o2")
+        vn("o2", "ps20")
+        did(v.tensor_tensor_scan(T.ps2[:, 8:PB], T.o2[:], T.o2[:], 0.0, Op.add, Op.max), "ps2")
+        vn("ps2")
+        did(v.tensor_copy(T.cl2[:], T.ps2[:, PB - 2:PB]), "cl2")
+        gn("cl2")
+        write([c for c in dests if c != core], T.ld2[:, 2 * r:2 * r + 2], T.cl2[:], "c2", cmask(core))
+        pn("o2", "ps2")
+        did(pe.matmul(T.p0[:, 0:256], T.u1[:], T.o2[:], True, False), "W2")
+        did(pe.matmul(T.p0[:, 0:256], T.bo[:], T.ps2[:, 7:PB - 1], False, True), "W2")
+        vn("W2")
+        did(v.tensor_tensor(T.m2[:], T.p0[:, 0:256], T.o2[:], Op.mult), "m2")
+        targets(lambda s: T.m2[:, s], lambda s: T.o2[:, s], ["m2", "o2"], T.p1, "tg2")
+        scatter(T.p1, T.tf[:, 32:64], T.to2, T.win2, "tg2", "win2", "sc2")
+        merge(T.win1, T.p7, "sc1", "mg1")
+        merge(T.win2, T.p5, "sc2", "mg2")
+    else:
+        first_lists()
+        merge(T.win1, T.p7, "sc1", "mg1")
+    offsets(T.p7, T.off1, "mg1", "off1")
+    if isr:
+        pack(v, "v", [c for c in calls if c[1:] == (0, dloc)])
+    if asks:
+        offsets(T.p5, T.off2, "mg2", "off2")
+    elif isr:
+        list_constants()
+
+    if isr:
+        last_list()
+        pack(sa, "a", sorted((c for c in calls if c[2] != dloc or c[1]), key=lambda c: (c[2] == dloc, c)))
+    else:
+        onvec = lambda c: c[1] == 0 if asks else c[2] == 0
+        pack(v, "v", [c for c in calls if onvec(c)])
+        pack(sa, "a", [c for c in calls if not onvec(c)])
+    for h in (0, 1):
+        for d in (0, 1):
+            if dests[d] != core:
+                n = 2 * HB * (2 * h + d)
+                gn("pack%d%d" % (h, d))
+                write([dests[d]], PK[h][:, pos(r):pos(r) + width], T.ob[:, n:n + width], "pin%d" % h, pmask(core))
+
+    if isr:
+        inn = sum(bits(pmask(server[X, q])) for q in range(N) if q != r)
+        for h in (0, 1):
+            for q, k, a in ((v, "v", 0), (sa, "a", CAP // 2)):
+                need(q, k, "offF", "zero", "pack%d%d" % (h, dloc))
+                q.wait_ge(T.sem["pin%d" % h], inn)
+                for kk in (2 * h, 2 * h + 1):
+                    o = CAP * kk + a
+                    src = PK[h][:, :].indirect(T.offF[:, o // 16:o // 16 + CAP // 32])
+                    out = T.ys[:, o:o + CAP // 2]
+                    did(v.tensor_copy(out, src) if k == "v" else sa.activation(out, src, Act.Copy), "ys%d" % kk)
+        for kk in range(EL):
             need(sy, "y", "ys%d" % kk)
             did(sy.dma_start(T.y[:, CAP * kk:CAP * kk + CAP], T.ys[:, CAP * kk:CAP * kk + CAP]), "y", 16)
         need(sy, "y", "y")

from concourse.bass import DstId, RemoteDMATransfer
from concourse.mybir import AluOpType as Op, ActivationFunctionType as Act

NC, N, NT, EL, CAP, CAPP = 128, 8, 4096, 4, 960, 256
FIRST2 = CAP // CAPP
NSEG = N + N - FIRST2
HB = EL // 2 * CAPP
pos = lambda q: HB * q + HB * max(0, q - FIRST2)
ZERO = HB * NSEG
PIECES = [[(0, 1184), (1184, 2240)], [(2240, 3216), (3216, 4096)]]
WHOLE = [(0, 2240), (2240, 4096)]
R0, RW = 2240, 1184
PB = 264
NTOK8, SLOTS = NT // 8, 8 * CAPP

SCRATCH = {"p%d" % _i: ("psum", [128, 512], "float32") for _i in range(8)}
for _d, _b in (
    ("bfloat16", dict(
        xw=NT, rl=2 * RW,
        pk0=ZERO + CAP, pk1=ZERO + CAP,
        ys=EL * CAP, ob=8 * HB,
        cl=4, ld1=4 * N, cl2=2, ld2=2 * N,
        colA=144, colG=128, colX=240, colT=256, colH=128, rg=1024, bo=128, rep=128, gt=128, u1=128, wd=144, wide=240, wideW=240,
        mapd=128, repq=1024, dat=NTOK8, lb=64, o1=1024, m1=1024, ps=4 * PB, ps2=PB, hh=256, o2=256, m2=256, thr=512,
        win1=NTOK8 + SLOTS, win2=NTOK8 + SLOTS, hl=60)),
    ("float32", dict(sc=64, trash=32, tf=64, cap=2 * NSEG, bq=NSEG + 1, db=NSEG, dl=NSEG, tb=30 * NSEG + 420)),
    ("int32", dict(le=64, pi=1, ia=8)),
    ("uint16", dict(to1=32, to2=32, off1=SLOTS // 16, off2=SLOTS // 16, offF=EL * CAP // 16)),
):
    SCRATCH.update({_n: ("sbuf", [128, _w], _d) for _n, _w in _b.items()})
SEMAPHORES = ["lst", "xin", "c1a", "c1b", "c2", "pin0", "pin1", "rel0", "rel1", "sent"] + ["s%d" % i for i in range(140)]


def plan(T, topo):
    cores = list(T.cores)
    chips = []
    for c in cores:
        if topo.chip(c) not in chips:
            chips.append(topo.chip(c))
    on = {}
    for c in range(NC):
        on.setdefault(topo.chip(c), []).append(c)
    server, relay, mrel = {}, {}, {}
    for X in chips:
        own = [c for c in cores if topo.chip(c) == X]
        cand = [c for c in on[X] if topo.die(c) != topo.die(own[0]) and all(topo.may_write(c, d) for d in cores if topo.chip(d) != X)]
        for i, c in enumerate(own):
            relay[c] = cand[i]
        free = sorted((c for c in on[X] if c not in own), key=lambda c: (topo.die(c) != topo.die(own[0]), c in cand))
        for r in sorted(range(N), key=lambda q: (not topo.same_plane(X, topo.chip(cores[q])), q)):
            server[X, r] = cores[r] if cores[r] in own else free.pop(0)
    for X in chips:
        M = [m for m in on if topo.mates(X, m)][0]
        far = [A for A in chips if A != X and not topo.same_plane(A, X)]
        for k, A in enumerate(far):
            for i, c in enumerate([c for c in cores if topo.chip(c) == A]):
                for part, s in enumerate((c, relay[c])):
                    own = [m for m in on[M] if topo.die(m) == topo.die(s) and topo.may_write(m, server[X, cores.index(c)])]
                    mrel[X, cores.index(c), part] = (own[i], k)
    return cores, chips, server, relay, mrel


def rank_program(g, core, T, topo):
    cores, chips, server, relay, mrel = plan(T, topo)
    X = topo.chip(core)
    bits = lambda m: bin(m).count("1")
    sent = [0]

    def write(dsts, out, in_, rsem, mask):
        ids = [topo.addr(d) for d in dsts]
        if len(dsts) == 1:
            g.remote_dma(out, in_, T.sem[rsem], T.sem.sent, pid=ids[0][1], routing_id=ids[0][0], dma_engine_mask=mask)
        elif dsts:
            g.remote_dma_fused([RemoteDMATransfer(dst_ids=[DstId(rid=a[0], pnc=a[1]) for a in ids], dma_engine_mask=mask, remote_sem=T.sem[rsem],
                                                  srcs=[in_], dsts=[out for _ in dsts])], local_sem=T.sem.sent)
        sent[0] += bits(mask) if dsts else 0

    if X not in chips:
        for k, q, Y, part in sorted((mrel[key][1], key[1], key[0], key[2]) for key in mrel if mrel[key][0] == core):
            a, b = PIECES[part][0]
            OFF = topo.mask(core, server[Y, q])
            g.wait_ge(T.sem["rel%d" % k], bits(OFF))
            write([server[Y, q]], T.xw[:, a:b], T.rl[:, RW * k:RW * k + b - a], "xin", OFF)
        if sent[0]:
            g.wait_ge(T.sem.sent, sent[0])
        return

    x = chips.index(X)
    r = [q for q in range(N) if server[X, q] == core][0]
    dests = [c for c in cores if topo.chip(c) == X]
    isr = core in dests
    dloc = dests.index(core) if isr else None
    asks = r >= FIRST2
    others = [Y for Y in chips if Y != X]
    ON = topo.mask(core, [c for c in dests if c != core][0])
    OFF = topo.mask(core, server[others[0], 0])
    HI = ON & ~OFF
    busy = lambda c: c in dests or c in [relay[d] for d in dests]
    cmask = lambda c: HI if busy(c) else ON
    v, pe, sa, sy = g.vector, g.tensor, g.scalar, g.sync

    num, cnt, seen = {}, {}, {}

    def did(ins, nm, n=1):
        if nm not in num:
            num[nm] = len(num)
            cnt[nm] = 0
        ins.then_inc(T.sem["s%d" % num[nm]], n)
        cnt[nm] += n

    def need(q, k, *names):
        for nm in names:
            if seen.get((k, nm)) != cnt[nm]:
                q.wait_ge(T.sem["s%d" % num[nm]], cnt[nm])
                seen[k, nm] = cnt[nm]

    def vn(*a): need(v, "v", *a)
    def pn(*a): need(pe, "p", *a)
    def gn(*a): need(g, "g", *a)

    if isr:
        did(sy.dma_start(T.le[:, 0:32], T.e1[:]), "le", 16)
        did(sa.dma_start(T.le[:, 32:64], T.e2[:]), "le", 16)
        for i, (p, j) in enumerate([(1, 0), (1, 1), (0, 0), (0, 1)]):
            a, b = PIECES[p][j]
            did((sy if i % 2 == 0 else sa).dma_start(T.xw[:, a:b], T.x[:, a:b]), "x%d%d" % (p, j), 16)

    row = dict(allow_small_or_imprecise_dtypes=True)
    did(g.iota(T.pi[:], [[0, 1]], 0, 1), "pi")
    did(g.iota(T.colX[:], [[1, 240]], -112, 0, **row), "colX")
    did(g.iota(T.colA[:], [[0, 9], [1, 16]], 0, 0, **row), "colA")
    did(g.iota(T.colG[:], [[1, 8], [0, 16]], 0, 0, **row), "colG")
    did(g.iota(T.colT[:], [[1, 256]], 1, 0, **row), "colT")

    def by_mates(q, part, src):
        via = [mrel[Y, q, part] for Y in others if (Y, q, part) in mrel]
        a, b = PIECES[part][0]
        k = via[0][1]
        write([m[0] for m in via], T.rl[:, RW * k:RW * k + b - a], src, "rel%d" % k, OFF)

    def direct(q, part, src):
        a, b = PIECES[part][1]
        write([server[Y, q] for Y in others if (Y, q, part) in mrel], T.xw[:, a:b], src, "xin", OFF)

    def in_plane(q, part, src):
        a, b = WHOLE[part]
        write([server[Y, q] for Y in others if (Y, q, part) not in mrel], T.xw[:, a:b], src, "xin", OFF)

    X_ = lambda ab: T.xw[:, ab[0]:ab[1]]
    R_ = lambda ab: T.rl[:, ab[0] - R0:ab[1] - R0]
    if isr:
        gn("le")
        write([server[Y, r] for Y in others], T.le[:], T.le[:], "lst", OFF)
        for j in (0, 1):
            gn("x1%d" % j)
            write([relay[core]], R_(PIECES[1][j]), X_(PIECES[1][j]), "rel%d" % j, HI)
        gn("x00")
        by_mates(r, 0, X_(PIECES[0][0]))
        gn("x01")
        direct(r, 0, X_(PIECES[0][1]))
        in_plane(r, 0, X_(WHOLE[0]))
        did(g.iota(T.colH[:], [[1, 4], [0, 32]], EL * dloc, 0, **row), "colH")
    passes = [cores.index(c) for c in dests if relay[c] == core]
    if passes:
        g.wait_ge(T.sem.rel0, bits(HI))
        by_mates(passes[0], 1, R_(PIECES[1][0]))

    S = lambda i, n=1: T.sc[:, i:i + n]
    TH0, TH, PMG, EK, ISQ = 24, 28, 32, 40, 44
    B30 = lambda s, n=1: T.tb[:, 30 * s:30 * s + 30 * n]
    T6, T3, TA, TC, TD, TE, PG = 13, 19, 22, 23, 24, 25, 26
    I8 = T.colX[:, 112:120]
    vn("pi")
    did(v.tensor_scalar(T.ia[:, 0:1], T.pi[:], 15, None, Op.bitwise_and), "ia")
    did(v.tensor_scalar(T.ia[:, 1:2], T.pi[:], 4, None, Op.arith_shift_right), "ia")
    did(v.tensor_scalar(T.ia[:, 2:3], T.pi[:], 0, None, Op.arith_shift_right), "ia")
    if isr:
        did(v.tensor_scalar(T.ia[:, 3:4], T.pi[:], 4, 1, Op.arith_shift_right, Op.bitwise_and), "ia")
        did(v.tensor_scalar(T.ia[:, 4:5], T.pi[:], 5, 1, Op.arith_shift_right, Op.bitwise_and), "ia")
    vn("ia")
    did(v.tensor_copy(S(0, 3), T.ia[:, 0:3]), "sc")
    vn("sc", "colX", "colA", "colG")
    did(v.tensor_scalar(S(PMG, 8), I8, -1.0, S(2), Op.mult, Op.add), "pmg")
    did(v.tensor_scalar(S(EK, 4), T.colX[:, 112:144:8], S(1), None, Op.add), "ek")
    vn("pmg")
    for q in range(8):
        did(v.tensor_scalar(T.rg[:, 128 * q:128 * q + 128], T.colA[:, 0:128], 8.0, S(PMG + q), Op.mult, Op.is_equal), "rg")
    did(v.memset(T.ps[:], 0.0), "ps0")
    if asks:
        did(v.memset(T.ps2[:], 0.0), "ps20")
    did(v.tensor_scalar(T.bo[:], T.colG[:], S(1), None, Op.is_equal), "bo")
    did(v.tensor_scalar(T.gt[:], T.colA[:, 0:128], S(0), None, Op.is_gt), "gt")
    did(v.tensor_scalar(T.rep[:], T.colA[:, 0:128], S(0), None, Op.is_equal), "rep")
    vn("bo", "gt")
    did(v.tensor_tensor(T.u1[:], T.bo[:], T.gt[:], Op.mult), "u1")
    did(v.tensor_scalar(S(8), S(1), 2.0, float(CAPP), Op.add, Op.mult), "sc8")
    did(v.tensor_scalar(S(3), S(0), 0.0, None, Op.is_equal), "sc3")
    did(v.tensor_scalar(S(4), S(0), 1.0, None, Op.is_equal), "sc4")
    did(v.tensor_scalar(S(5), S(0), 2.0, None, Op.is_lt), "sc5")
    did(v.tensor_scalar(T.wide[:], T.colX[:], S(0), None, Op.is_equal), "wide")
    vn("sc8")
    did(v.tensor_scalar(T.wideW[:], T.colX[:], S(0), S(8), Op.is_equal, Op.mult), "wide")
    did(v.tensor_scalar(T.trash[:], T.colX[:, 112:144], 16.0, S(0), Op.mult, Op.add), "trash")
    vn("sc4", "sc5")
    did(v.tensor_scalar(S(6), S(1), float(NTOK8), S(4), Op.mult, Op.mult), "sc6")
    did(v.tensor_scalar(T.wd[:], T.colA[:], 15.0, S(5), Op.is_equal, Op.mult), "wd")
    vn("sc6")
    did(v.tensor_scalar(S(7), S(4), 256.0, S(6), Op.mult, Op.add), "sc7")
    vn("colT", "sc3", "sc7")
    did(v.tensor_scalar(T.dat[:, 0:256], T.colT[:], S(3), S(6), Op.mult, Op.add), "dat")
    did(v.tensor_scalar(T.dat[:, 256:512], T.colT[:], S(3), S(7), Op.mult, Op.add), "dat")
    did(v.memset(T.win1[:, NTOK8:], 0.0), "win1")

    if isr:
        vn("le")
    else:
        v.wait_ge(T.sem.lst, bits(OFF))
    did(v.tensor_copy(T.lb[:], T.le[:]), "lb")
    pn("lb", "rg")
    for q in range(8):
        did(pe.matmul(T.p0[:, 32 * q:32 * q + 32], T.rg[:, 128 * q:128 * q + 128], T.lb[:, 0:32], True, True), "E1")
    if asks:
        for q in range(8):
            did(pe.matmul(T.p1[:, 32 * q:32 * q + 32], T.rg[:, 128 * q:128 * q + 128], T.lb[:, 32:64], True, True), "E2")
    rounds = [x] + [i for i in range(4) if i != x]
    ocol = lambda i: (256 * i, 256 * i + 256)
    vn("E1", "ek")
    for i in rounds:
        a, b = ocol(i)
        did(v.tensor_scalar(T.o1[:, a:b], T.p0[:, 0:256], S(EK + i), None, Op.is_equal), "o1_%d" % i)
    vn("ps0")
    for i in rounds:
        a, b = ocol(i)
        vn("o1_%d" % i)
        did(v.tensor_tensor_scan(T.ps[:, PB * i + 8:PB * i + PB], T.o1[:, a:b], T.o1[:, a:b], 0.0, Op.add, Op.max), "ps_%d" % i)
    vn(*["ps_%d" % i for i in rounds])
    did(v.tensor_copy(T.cl[:], T.ps[:, PB - 1::PB]), "cl")

    gn("cl")
    lat = [server[X, q] for q in range(N) if q > r and (q >= FIRST2 or server[X, q] in dests)]
    write(lat, T.ld1[:, 4 * r:4 * r + 4], T.cl[:], "c1a", cmask(core))
    write([c for c in dests if cores.index(c) < r], T.ld1[:, 4 * r:4 * r + 4], T.cl[:], "c1b", cmask(core))
    landed = lambda qs: sum(bits(cmask(server[X, q])) for q in qs)
    if passes:
        g.wait_ge(T.sem.rel1, bits(HI))
        direct(passes[0], 1, R_(PIECES[1][1]))
        in_plane(passes[0], 1, R_(WHOLE[1]))

    bank = {}
    pn("u1", "bo")
    use = rounds if asks else rounds[:1]
    for j, i in enumerate(use):
        a, b = ocol(i)
        bank[i] = [T.p2, T.p3][j // 2][:, 256 * (j % 2):256 * (j % 2) + 256]
        pn("o1_%d" % i)
        did(pe.matmul(bank[i], T.u1[:], T.o1[:, a:b], True, False), "W%d" % (j // 2))
        pn("ps_%d" % i)
        did(pe.matmul(bank[i], T.bo[:], T.ps[:, PB * i + 7:PB * i + PB - 1], False, True), "W%d" % (j // 2))
    if asks:
        vn("E2")
        did(v.tensor_scalar(T.hh[:], T.p1[:, 0:256], S(EK + x), 1048576.0, Op.not_equal, Op.mult), "hh")
    for j, i in enumerate(use):
        a, b = ocol(i)
        vn("W%d" % (j // 2))
        did(v.tensor_tensor(T.m1[:, a:b], bank[i], T.o1[:, a:b], Op.mult), "m1_%d" % i)
    if asks:
        did(v.memset(T.win2[:, NTOK8:], 0.0), "win2")

    def targets(m, o, names, ps, key):
        pn("wide", *names)
        for q in range(8):
            s = slice(32 * q, 32 * q + 32)
            w = slice(112 - 16 * q, 240 - 16 * q)
            did(pe.matmul(ps[:, 0:32], T.wide[:, w], m(s), q == 0, False), key)
            did(pe.matmul(ps[:, 0:32], T.wideW[:, w], o(s), False, q == 7), key)

    def scatter(ps, tf, to, win, tkey, wkey, key):
        vn(tkey, "trash")
        did(v.tensor_tensor(tf, ps[:, 0:32], T.trash[:], Op.max), key + "f")
        vn(key + "f")
        did(v.tensor_copy(to[:], tf), key + "o")
        vn(key + "o", wkey, "dat")
        did(v.tensor_copy(win[:, :].indirect(to[:, :]), T.dat[:]), key)

    def merge(win, ps, key, mkey):
        pn("wd", key)
        for a in range(16):
            did(pe.matmul(ps[:, 0:SLOTS // 16], T.wd[:, 15 - a:143 - a], win[:, NTOK8 + a::16], a == 0, a == 15), mkey)

    def offsets(ps, off, mkey, okey):
        vn(mkey)
        did(v.tensor_scalar(off[:], ps[:, 0:SLOTS // 16], -1.0, 0.0, Op.add, Op.max), okey)

    def first_lists():
        a0 = 256 * x
        targets(lambda s: T.m1[:, a0 + s.start:a0 + s.stop], lambda s: T.o1[:, a0 + s.start:a0 + s.stop], ["m1_%d" % x, "o1_%d" % x], T.p6, "tg1")
        scatter(T.p6, T.tf[:, 0:32], T.to1, T.win1, "tg1", "win1", "sc1")

    PK = (T.pk0, T.pk1)
    width = (2 if asks else 1) * HB
    calls = [(h, t, d) for h in (0, 1) for t in ((0, 1) if asks else (0,)) for d in (0, 1)]
    pmask = lambda c: HI if c in dests else ON

    def pack(q, k, todo):
        if todo and isr:
            need(q, k, "x00", "x01", "x10", "x11")
        elif todo:
            q.wait_ge(T.sem.xin, bits(OFF) * (2 if topo.same_plane(X, topo.chip(cores[r])) else 4))
        for h, t, d in todo:
            need(q, k, ("off1", "off2")[t])
            o = 64 * d + 32 * h
            src = T.xw[:, 0:NT].indirect((T.off1, T.off2)[t][:, o:o + HB // 16])
            s = HB * t + (pos(r) if dests[d] == core else 2 * HB * (2 * h + d))
            out = (PK[h] if dests[d] == core else T.ob)[:, s:s + HB]
            did(v.tensor_copy(out, src) if k == "v" else sa.activation(out, src, Act.Copy), "pack%d%d" % (h, d))

    def list_constants():
        did(v.memset(T.pk0[:, ZERO:], 0.0), "zero")
        did(v.memset(T.pk1[:, ZERO:], 0.0), "zero")
        did(v.memset(T.cap[:, 0:NSEG], float(CAP)), "cap")
        first = [pos(q) for q in range(N)] + [pos(q) + HB for q in range(FIRST2, N)] + [ZERO]
        step = [first[s + 1] - first[s] for s in range(NSEG)]
        s = 0
        while s < NSEG:
            e = s
            while e < NSEG and step[e] == step[s]:
                e += 1
            did(v.memset(T.cap[:, NSEG + s:NSEG + e], float(step[s])), "cap")
            s = e
        did(v.memset(T.bq[:, 0:1], 0.0), "bq0")
        did(v.tensor_copy(S(11), T.ia[:, 3:4]), "sc11")
        did(v.tensor_scalar(S(10), T.ia[:, 4:5], float(CAPP), None, Op.mult), "sc10")
        vn("sc11", "colH")
        did(v.tensor_scalar(S(9), S(11), float(CAP // 2), S(0), Op.mult, Op.add), "sc9")
        did(v.tensor_scalar(T.mapd[:], T.colH[:], S(1), None, Op.is_equal), "mapd")
        did(v.tensor_scalar(S(ISQ, 8), I8, S(1), None, Op.is_equal), "isq")
        vn("sc9", "sc10", "isq", "rep")
        did(v.tensor_scalar(B30(PG), T.colX[:, 112:142], 16.0, S(9), Op.mult, Op.add), "pg")
        for q in range(8):
            did(v.tensor_scalar(T.repq[:, 128 * q:128 * q + 128], T.rep[:], S(ISQ + q), None, Op.mult), "repq")

    def last_list():
        if r and not asks:
            pe.wait_ge(T.sem.c1a, landed(range(r)))
        if r < N - 1:
            pe.wait_ge(T.sem.c1b, landed(range(r + 1, N)))
        pe.wait_ge(T.sem.c2, landed(q for q in range(FIRST2, N) if q != r))
        pn("mapd", "cl", *(["m1_%d" % i for i in use] + (["cl2"] if asks else [])))
        for q in range(N):
            src = T.cl[:, x:x + 1] if q == r else T.ld1[:, 4 * q + x:4 * q + x + 1]
            did(pe.matmul(T.p2[:, q:q + 1], T.mapd[:], src, True, True), "ns")
        for q in range(FIRST2, N):
            src = T.cl2[:, 1:2] if q == r else T.ld2[:, 2 * q + 1:2 * q + 2]
            did(pe.matmul(T.p2[:, N + q - FIRST2:N + q - FIRST2 + 1], T.mapd[:], src, True, True), "ns")
        vn("ns", "cap", "bq0")
        did(v.tensor_tensor_scan(T.bq[:, 1:NSEG + 1], T.p2[:, 0:NSEG], T.cap[:, 0:NSEG], 0.0, Op.add, Op.min), "bq")
        vn("bq")
        did(v.tensor_tensor(T.db[:], T.bq[:, 1:NSEG + 1], T.bq[:, 0:NSEG], Op.subtract), "db")
        vn("db")
        did(v.tensor_tensor(T.dl[:], T.cap[:, NSEG:2 * NSEG], T.db[:], Op.subtract), "dl")
        vn("dl")
        L = NSEG - 1
        did(v.tensor_scalar(S(12), T.dl[:, L:L + 1], S(10), None, Op.subtract), "dz")
        vn("dz", "pg")
        for s in range(NSEG):
            did(v.tensor_scalar(B30(s), B30(PG), T.bq[:, s + 1:s + 2], T.dl[:, s:s + 1] if s < L else S(12), Op.is_ge, Op.mult), "tb")
        did(v.tensor_scalar(B30(TA), B30(PG), S(10), None, Op.add), "ta")
        vn("tb", "ta")
        did(v.tensor_tensor(B30(T6, 6), B30(0, 6), B30(6, 6), Op.add), "t6")
        did(v.tensor_tensor(B30(TC), B30(TA), B30(12), Op.add), "tc")
        vn("t6")
        did(v.tensor_tensor(B30(T3, 3), B30(T6, 3), B30(T6 + 3, 3), Op.add), "t3")
        vn("t3", "tc")
        did(v.tensor_tensor(B30(TD), B30(T3), B30(T3 + 1), Op.add), "td")
        did(v.tensor_tensor(B30(TE), B30(T3 + 2), B30(TC), Op.add), "te")
        vn("td", "te")
        did(v.tensor_tensor(B30(TA), B30(TD), B30(TE), Op.add), "src")
        vn("src")
        did(v.tensor_copy(T.hl[:, 0:30], B30(TA)), "hb")
        vn("hb")
        did(v.tensor_tensor(T.hl[:, 30:60], B30(TA), T.hl[:, 0:30], Op.subtract), "lo")
        pn("hb", "lo", "repq")
        for q in range(8):
            for i in (0, 1):
                did(pe.matmul(T.p3[:, 30 * q:30 * q + 30], T.repq[:, 128 * q:128 * q + 128], T.hl[:, 30 * i:30 * i + 30], i == 0, i == 1), "of")
        vn("of")
        did(v.tensor_copy(T.offF[:], T.p3[:, 0:240]), "offF")

    if asks:
        pn("rep")
        for j, i in enumerate(rounds):
            a, b = ocol(i)
            pn("m1_%d" % i)
            did(pe.matmul(T.p4[:, 0:256], T.rep[:], T.m1[:, a:b], j == 0, False), "D")
        first_lists()
        if isr:
            list_constants()
        before = [q for q in range(N) if q < r]
        pe.wait_ge(T.sem.c1a, landed(before))
        for q in before:
            did(pe.matmul(T.p5[:, 0:4], T.bo[:], T.ld1[:, 4 * q:4 * q + 4], q == 0, q == before[-1]), "base")
        vn("base")
        did(v.tensor_scalar(S(TH0, 4), T.p5[:, 0:4], -float(CAP), 0.0, Op.add, Op.min), "th0")
        vn("th0")
        did(v.tensor_scalar(S(TH, 4), S(TH0, 4), -float(CAPP), None, Op.max), "th")
        vn("th", "rep")
        for i in rounds:
            did(v.tensor_scalar(T.thr[:, 128 * i:128 * i + 128], T.rep[:], S(TH + i), None, Op.mult), "thr%d" % i)
        for j, i in enumerate(rounds):
            a, b = ocol(i)
            pn("thr%d" % i)
            did(pe.matmul(T.p4[:, 0:256], T.thr[:, 128 * i:128 * i + 128], T.o1[:, a:b], False, j == 3), "D")
        vn("D", "hh")
        did(v.tensor_tensor(T.o2[:], T.p4[:, 0:256], T.hh[:], Op.is_ge), "o2")
        vn("o2", "ps20")
        did(v.tensor_tensor_scan(T.ps2[:, 8:PB], T.o2[:], T.o2[:], 0.0, Op.add, Op.max), "ps2")
        vn("ps2")
        did(v.tensor_copy(T.cl2[:], T.ps2[:, PB - 2:PB]), "cl2")
        gn("cl2")
        write([c for c in dests if c != core], T.ld2[:, 2 * r:2 * r + 2], T.cl2[:], "c2", cmask(core))
        pn("o2", "ps2")
        did(pe.matmul(T.p0[:, 0:256], T.u1[:], T.o2[:], True, False), "W2")
        did(pe.matmul(T.p0[:, 0:256], T.bo[:], T.ps2[:, 7:PB - 1], False, True), "W2")
        vn("W2")
        did(v.tensor_tensor(T.m2[:], T.p0[:, 0:256], T.o2[:], Op.mult), "m2")
        targets(lambda s: T.m2[:, s], lambda s: T.o2[:, s], ["m2", "o2"], T.p1, "tg2")
        scatter(T.p1, T.tf[:, 32:64], T.to2, T.win2, "tg2", "win2", "sc2")
        merge(T.win1, T.p7, "sc1", "mg1")
        merge(T.win2, T.p5, "sc2", "mg2")
    else:
        first_lists()
        merge(T.win1, T.p7, "sc1", "mg1")
    offsets(T.p7, T.off1, "mg1", "off1")
    if isr:
        pack(v, "v", [c for c in calls if c[1:] == (0, dloc)])
    if asks:
        offsets(T.p5, T.off2, "mg2", "off2")
    elif isr:
        list_constants()

    if isr:
        last_list()
        pack(sa, "a", sorted((c for c in calls if c[2] != dloc or c[1]), key=lambda c: (c[2] == dloc, c)))
    else:
        onvec = lambda c: c[1] == 0 if asks else c[2] == 0
        pack(v, "v", [c for c in calls if onvec(c)])
        pack(sa, "a", [c for c in calls if not onvec(c)])
    for h in (0, 1):
        for d in (0, 1):
            if dests[d] != core:
                n = 2 * HB * (2 * h + d)
                gn("pack%d%d" % (h, d))
                write([dests[d]], PK[h][:, pos(r):pos(r) + width], T.ob[:, n:n + width], "pin%d" % h, pmask(core))

    if isr:
        inn = sum(bits(pmask(server[X, q])) for q in range(N) if q != r)
        for h in (0, 1):
            for q, k, a in ((v, "v", 0), (sa, "a", CAP // 2)):
                need(q, k, "offF", "zero", "pack%d%d" % (h, dloc))
                q.wait_ge(T.sem["pin%d" % h], inn)
                for kk in (2 * h, 2 * h + 1):
                    o = CAP * kk + a
                    src = PK[h][:, :].indirect(T.offF[:, o // 16:o // 16 + CAP // 32])
                    out = T.ys[:, o:o + CAP // 2]
                    did(v.tensor_copy(out, src) if k == "v" else sa.activation(out, src, Act.Copy), "ys%d" % kk)
        for kk in range(EL):
            need(sy, "y", "ys%d" % kk)
            did(sy.dma_start(T.y[:, CAP * kk:CAP * kk + CAP], T.ys[:, CAP * kk:CAP * kk + CAP]), "y", 16)
        need(sy, "y", "y")
    g.wait_ge(T.sem.sent, sent[0])
    gn(*[nm for nm in num if not [k for k, m in seen if m == nm and seen[k, m] == cnt[nm]]])
